import numpy as np
import ml_dtypes


def mxq(x, axis, fmt="e4m3"):
    dtype, down = {"e4m3": (ml_dtypes.float8_e4m3fn, 7), "e5m2": (ml_dtypes.float8_e5m2, 14)}[fmt]
    v = np.moveaxis(np.asarray(x, np.float32).astype(ml_dtypes.bfloat16).astype(np.float64), axis, -1)
    blocks = v.reshape(v.shape[:-1] + (-1, 32))
    amax = np.abs(blocks).max(-1, keepdims=True)
    byte = np.maximum(np.where(amax > 0, np.frexp(amax)[1] - 1 + 127, 0) - down, 1)
    scale = np.exp2(byte - 127.0)
    codes = (blocks / scale).astype(np.float32).astype(dtype).astype(np.float64)
    return np.moveaxis((codes * scale).reshape(v.shape), -1, axis)


WIDE = False


def mx_kscale(k):
    if not WIDE:
        return np.ones(k)
    levels = np.array([30, -30])
    if k % 512:
        return np.exp2(np.random.permutation(np.resize(levels, k // 32))).repeat(32)
    a = np.empty((k // 512, 16))
    for p in range(k // 512):
        a[p, :8] = np.random.permutation(np.resize(levels, 8))
        for g in range(8):
            far = levels[np.abs(levels - a[p, g]) >= 10]
            a[p, g + 8] = far[np.random.randint(len(far))]
    return np.exp2(a.ravel()).repeat(32)


BF16 = ml_dtypes.bfloat16


def bf(x):
    return np.asarray(x, np.float32).astype(BF16)


def f64(x):
    return np.asarray(x).astype(np.float64)


E2M1 = np.array([0.0, 0.5, 1.0, 1.5, 2.0, 3.0, 4.0, 6.0, -0.0, -0.5, -1.0, -1.5, -2.0, -3.0, -4.0, -6.0])


def pack_weight(w, fmt):
    k, n = w.shape
    w = f64(bf(w)).reshape(k // 32, 32, n)
    amax = np.abs(w).max(1)
    if fmt in ("e4m3", "e5m2"):
        byte = np.frexp(amax)[1] - 1 + 127 - (7 if fmt == "e4m3" else 14)
    else:
        mant, ex = np.frexp(amax / 6.0)
        byte = np.where(mant > 0.5, ex, ex - 1) + 127
    byte = np.clip(np.where(amax > 0, byte, 1), 1, 254)
    scaled = (w * np.exp2(127.0 - byte)[:, None, :]).reshape(k, n).astype(np.float32)
    by_word = np.ascontiguousarray(scaled.reshape(k // 512, 128, 4, n).transpose(0, 1, 3, 2))
    if fmt in ("e4m3", "e5m2"):
        words = by_word.astype(ml_dtypes.float8_e4m3fn if fmt == "e4m3" else ml_dtypes.float8_e5m2).view(np.uint8)
    else:
        c = by_word.astype(ml_dtypes.float4_e2m1fn).view(np.uint8) & 0xF
        words = c[..., 0::2] | (c[..., 1::2] << 4)
    return np.ascontiguousarray(words), np.ascontiguousarray(byte.astype(np.uint8).reshape(k // 512, 16, n))


def unpack_weight(words, scales, fmt):
    g, p, n, _ = words.shape
    if fmt in ("e4m3", "e5m2"):
        vals = np.ascontiguousarray(words).view(ml_dtypes.float8_e4m3fn if fmt == "e4m3" else ml_dtypes.float8_e5m2).astype(np.float64)
    else:
        nib = np.empty((g, p, n, 4), np.uint8)
        nib[..., 0::2] = words & 0xF
        nib[..., 1::2] = words >> 4
        vals = E2M1[nib]
    vals = vals * np.repeat(np.exp2(scales.astype(np.float64) - 127.0), 8, axis=1)[..., None]
    return vals.transpose(0, 1, 3, 2).reshape(g * 512, n)


T, D, N, O, R = 2048, 1024, 1536, 1024, 128

ALPHA = 16.0


def setup_inputs():
    c, s, u = mx_kscale(D), mx_kscale(O), mx_kscale(T)
    x = np.random.standard_normal((T, D)) * c * u[:, None]
    a_down = np.random.standard_normal((D, R)) / np.sqrt(D) / c[:, None]
    G = np.random.standard_t(5, (O, T)) * s[:, None] / u
    g_words, g_scales = pack_weight(G, "e5m2")
    w = np.random.standard_normal((N, O)) / np.sqrt(O) / s
    y = np.random.standard_normal((T, N))
    sg = 1.0 / (1.0 + np.exp(-y))
    slope = sg * (1.0 + y * (1.0 - sg))
    return {"x": bf(x),
            "a_down": bf(a_down),
            "g_words": g_words,
            "g_scales": g_scales,
            "w": bf(w),
            "slope": bf(slope),
            "acc": bf(2.0 * np.random.standard_normal((R, N)))}


def reference(x, a_down, g_words, g_scales, w, slope, acc):
    G = unpack_weight(g_words, g_scales, "e5m2")
    h = mxq(f64(x), 1, "e4m3") @ mxq(f64(a_down), 0, "e4m3")
    back = G.T @ mxq(f64(w), 1, "e4m3").T
    dy = back * f64(slope)
    db = mxq(h, 0, "e4m3").T @ mxq(dy, 0, "e5m2")
    return f64(acc) + (ALPHA / R) * db

@@ -1,0 +1,343 @@
+from contextlib import ExitStack
+
+import concourse.mybir as mybir
+from concourse.masks import make_identity
+
+F32 = mybir.dt.float32
+BF16 = mybir.dt.bfloat16
+I32 = mybir.dt.int32
+U32 = mybir.dt.uint32
+U8 = mybir.dt.uint8
+E4M3 = mybir.dt.float8_e4m3fn_x4
+E5M2 = mybir.dt.float8_e5m2_x4
+MULT = mybir.AluOpType.mult
+ADD = mybir.AluOpType.add
+
+T, D, N, O, R = 2048, 1024, 1536, 1024, 128
+FLOPS = 2 * (T * D * R + O * T * N + T * R * N)
+
+P = 128
+KP = 512
+GROUPS = T // KP
+CHUNKS = N // 512
+KG = O // KP
+SCALE = 16.0 / 128.0
+
+
+def tile_lora_up_factor_gradient_e3_kernel(tc, x, a_down, g_words, g_scales, w, slope, acc, out):
+    nc = tc.nc
+    units = [(g, c) for c in range(CHUNKS) for g in range(GROUPS)]
+
+    with ExitStack() as ctx:
+        keep = ctx.enter_context(tc.tile_pool(name="keep", bufs=1))
+        ring = ctx.enter_context(tc.tile_pool(name="ring", bufs=2))
+        psum = ctx.enter_context(tc.psum_pool(name="psum", bufs=1))
+        ctx.enter_context(tc.manual_schedule())
+
+        w_raw = {}
+
+        def load_w(c, kg, halves):
+            if (c, kg) not in w_raw:
+                w_raw[c, kg] = ring.tile([P, 4, KP], BF16, name="w_raw", bufs=4, align_bytes=64)
+            t = w_raw[c, kg]
+            src = w[512 * c : 512 * (c + 1), KP * kg : KP * (kg + 1)].rearrange("(r p) k -> p r k", p=P)
+            for h in halves:
+                nc.sync.dma_start(out=t[:, h, :], in_=src[:, h, :])
+
+        g_flat = g_words.rearrange("k p n t -> k p (n t)")
+        g_raw = {}
+
+        def load_g(g):
+            t = ring.tile([P, KG, KP], I32, name="g_raw", bufs=2, align_bytes=64)
+            src = g_flat[:, :, 4 * KP * g : 4 * KP * (g + 1)].bitcast(I32).rearrange("k p n -> p k n")
+            nc.sync.dma_start(out=t[:], in_=src)
+            g_raw[g] = t
+
+        x_raw = {}
+
+        def load_x(g):
+            t = ring.tile([P, 4, D], BF16, name="x_raw", bufs=2, align_bytes=64)
+            src = x[KP * g : KP * (g + 1), :].rearrange("(j t b) d -> b j t d", t=4, b=4)
+            for b in range(4):
+                nc.sync.dma_start(out=t[b:P:4, :, :], in_=src[b])
+            x_raw[g] = t
+
+        slopes = {}
+
+        def load_slope(u):
+            g, c = units[u]
+            t = ring.tile([P, 4, 512], BF16, name="slope_sb", bufs=6, align_bytes=64)
+            src = slope[KP * g : KP * (g + 1), 512 * c : 512 * (c + 1)].rearrange("(j t b) n -> b j t n", t=4, b=4)
+            for b in range(4):
+                nc.sync.dma_start(out=t[b:P:4, :, :], in_=src[b])
+            slopes[u] = t
+
+        gs_raw = keep.tile([P, KG, T // 4], I32, name="gs_raw", align_bytes=64)
+        nc.vector.memset(gs_raw[:], 0)
+        ident = keep.tile([P, P], F32, name="ident", align_bytes=64)
+        make_identity(nc, ident[:])
+
+        def load_gs():
+            src = g_scales.bitcast(I32)
+            for q in range(4):
+                nc.sync.dma_start(
+                    out=gs_raw[32 * q : 32 * q + 4, :, :],
+                    in_=src[:, 4 * q : 4 * q + 4, :].rearrange("k r n -> r k n"),
+                )
+
+        a_raw = keep.tile([P, KG, 4, R], BF16, name="a_raw", align_bytes=64)
+        a_grp = keep.tile([P, KG, R, 4], BF16, name="a_grp", align_bytes=64)
+        a_codes = keep.tile([P, KG * R], U32, name="a_codes", align_bytes=64)
+        a_scales = keep.tile([P, KG * R], U8, name="a_scales", align_bytes=64)
+        acc_sb = keep.tile([P, N], BF16, name="acc_sb", align_bytes=64)
+
+        def load_a():
+            nc.sync.dma_start(out=a_raw[:], in_=a_down.rearrange("(k p j) r -> p k j r", p=P, j=4))
+
+        def load_acc():
+            nc.sync.dma_start(out=acc_sb[:], in_=acc[:, :])
+
+        w_codes = [keep.tile([P, KG, 512], U32, name=f"w_codes{c}", align_bytes=64) for c in range(CHUNKS)]
+        w_scales = [keep.tile([P, KG, 512], U8, name=f"w_scales{c}", align_bytes=64) for c in range(CHUNKS)]
+        gs = keep.tile([P, 4, KG * GROUPS * 32], I32, name="gs", align_bytes=64)
+
+        def tr_bank():
+            return psum.tile([P, 2, 2, P], F32, name="tr", bufs=4)
+
+        def unscramble(copy, dst, bank):
+            copy(
+                out=dst.rearrange("p n j -> p (n j)").bitcast(F32).rearrange("p (r m u) -> p r m u", r=2, u=2),
+                in_=bank[:].rearrange("p r u m -> p r m u"),
+            )
+
+        def transposes_w(c, kg, h):
+            bank = tr_bank()
+            for r in range(2):
+                words = w_raw[c, kg][:, 2 * h + r, :].bitcast(F32)
+                for u in range(2):
+                    nc.tensor.transpose(bank[:, r, u, :], words[:, u : 256 : 2], ident[:])
+            return bank
+
+        w_grp = {}
+
+        def turn_w(c, kg, h, copy):
+            if h == 0:
+                w_grp[c, kg] = ring.tile([P, 512, 4], BF16, name="w_grp", bufs=3, align_bytes=64)
+            unscramble(copy, w_grp[c, kg][:, 256 * h : 256 * (h + 1), :], transposes_w(c, kg, h))
+
+        def quant_w(c, kg):
+            nc.vector.quantize_mx(
+                out=w_codes[c][:, kg, :].bitcast(E4M3),
+                scales=w_scales[c][:, kg, :],
+                in_=w_grp[c, kg][:].rearrange("p n j -> p (n j)"),
+            )
+
+        x_grp = {}
+        x_codes = {}
+        x_scales = {}
+
+        def turn_x(g, h):
+            grp = ring.tile([P, 2, 256, 4], BF16, name="x_grp", bufs=3, align_bytes=64)
+            for i in range(2):
+                bank = tr_bank()
+                words = x_raw[g][:, 2 * h + i, :].bitcast(F32)
+                for kg in range(KG):
+                    for u in range(2):
+                        nc.tensor.transpose(bank[:, kg, u, :], words[:, 256 * kg + u : 256 * (kg + 1) : 2], ident[:])
+                unscramble(nc.scalar.copy, grp[:, i, :, :], bank)
+            x_grp[g, h] = grp
+
+        def quant_x(g, h):
+            if h == 0:
+                x_codes[g] = ring.tile([P, 4, KG * P], U32, name="x_codes", bufs=2, align_bytes=64)
+                x_scales[g] = ring.tile([P, 4, KG * P], U8, name="x_scales", bufs=2, align_bytes=64)
+            nc.vector.quantize_mx(
+                out=x_codes[g][:, 2 * h : 2 * h + 2, :].rearrange("p t c -> p (t c)").bitcast(E4M3),
+                scales=x_scales[g][:, 2 * h : 2 * h + 2, :].rearrange("p t c -> p (t c)"),
+                in_=x_grp[g, h][:].rearrange("p i n j -> p (i n j)"),
+            )
+
+        g_codes = {}
+
+        def order_g(g):
+            g_codes[g] = keep.tile([P, 4, KG * P], I32, name=f"g_codes{g}", align_bytes=64)
+            nc.vector.tensor_copy(
+                out=g_codes[g][:].rearrange("p t (kj b) -> p t kj b", b=4),
+                in_=g_raw[g][:].rearrange("p k n -> p (k n)").rearrange("p (kj t b) -> p t kj b", t=4, b=4),
+            )
+
+        y = {}
+
+        def back(u):
+            g, c = units[u]
+            banks = [psum.tile([P, 512], F32, name=f"back{t}", bufs=1) for t in range(4)]
+            for t, kg in [(t, kg) for t in range(4) for kg in range(KG)]:
+                col = 32 * (GROUPS * kg + g)
+                nc.tensor.matmul_mx(
+                    out=banks[t][:],
+                    lhsT=g_codes[g][:, t, P * kg : P * (kg + 1)].bitcast(E5M2),
+                    lhsT_scale=gs[:, t, col : col + 32].bitcast(U8),
+                    rhs=w_codes[c][:, kg, :].bitcast(E4M3),
+                    rhs_scale=w_scales[c][:, kg, :],
+                    start=(kg == 0),
+                    stop=(kg == KG - 1),
+                )
+            y[u] = ring.tile([P, P, 4, 4], F32, name="y", bufs=3, align_bytes=64)
+            for t in range(4):
+                nc.scalar.copy(out=y[u][:, :, t, :], in_=banks[t][:].rearrange("p (c i) -> p c i", i=4))
+
+        dy = {}
+
+        def mult(u):
+            dy[u] = ring.tile([P, 512, 4], BF16, name="dy", bufs=3, align_bytes=64)
+            nc.vector.tensor_tensor(
+                out=dy[u][:].rearrange("p (c i) t -> p c t i", i=4),
+                in0=y[u][:],
+                in1=slopes[u][:].rearrange("p t (c i) -> p c t i", i=4),
+                op=MULT,
+            )
+
+        dy_codes = {}
+        dy_scales = {}
+
+        def quant_dy(u):
+            dy_codes[u] = keep.tile([P, 512], U32, name=f"dy_codes{u}", align_bytes=64)
+            dy_scales[u] = keep.tile([P, 512], U8, name=f"dy_scales{u}", align_bytes=64)
+            nc.vector.quantize_mx(
+                out=dy_codes[u][:].bitcast(E5M2),
+                scales=dy_scales[u][:],
+                in_=dy[u][:].rearrange("p n t -> p (n t)"),
+            )
+
+        h_grp = {}
+        h_codes = {}
+        h_scales = {}
+
+        def h_product(g):
+            bank = psum.tile([P, 4, R], F32, name="tr", bufs=4)
+            for t in range(4):
+                for kg in range(KG):
+                    cols = slice(P * kg, P * (kg + 1))
+                    nc.tensor.matmul_mx(
+                        out=bank[:, t, :],
+                        lhsT=x_codes[g][:, t, cols].bitcast(E4M3),
+                        lhsT_scale=x_scales[g][:, t, cols],
+                        rhs=a_codes[:, cols].bitcast(E4M3),
+                        rhs_scale=a_scales[:, cols],
+                        start=(kg == 0),
+                        stop=(kg == KG - 1),
+                    )
+            h_grp[g] = ring.tile([P, R, 4], BF16, name="h_grp", bufs=2, align_bytes=64)
+            nc.scalar.copy(out=h_grp[g][:], in_=bank[:].rearrange("p t r -> p r t"))
+
+        def quant_h(g):
+            h_codes[g] = keep.tile([P, R], U32, name=f"h_codes{g}", align_bytes=64)
+            h_scales[g] = keep.tile([P, R], U8, name=f"h_scales{g}", align_bytes=64)
+            nc.vector.quantize_mx(
+                out=h_codes[g][:].bitcast(E4M3), scales=h_scales[g][:], in_=h_grp[g][:].rearrange("p r t -> p (r t)")
+            )
+
+        db = {}
+
+        def db_pass(c, g):
+            if g == 0:
+                db[c] = psum.tile([P, 512], F32, name="tr", bufs=4)
+            u = units.index((g, c))
+            nc.tensor.matmul_mx(
+                out=db[c][:],
+                lhsT=h_codes[g][:].bitcast(E4M3),
+                lhsT_scale=h_scales[g][:],
+                rhs=dy_codes[u][:].bitcast(E5M2),
+                rhs_scale=dy_scales[u][:],
+                start=(g == 0),
+                stop=(g == GROUPS - 1),
+            )
+
+        def combine(c, on_vector):
+            cols = slice(512 * c, 512 * (c + 1))
+            res = ring.tile([P, 512], F32, name="res", bufs=3, align_bytes=64)
+            if on_vector:
+                nc.vector.scalar_tensor_tensor(
+                    out=res[:], in0=db[c][:], scalar=SCALE, in1=acc_sb[:, cols], op0=MULT, op1=ADD
+                )
+            else:
+                scaled = ring.tile([P, 512], F32, name="scaled", bufs=2, align_bytes=64)
+                nc.scalar.mul(scaled[:], db[c][:], SCALE)
+                nc.gpsimd.tensor_tensor(out=res[:], in0=scaled[:], in1=acc_sb[:, cols], op=ADD)
+            nc.sync.dma_start(out=out[:, cols], in_=res[:])
+
+        halves = [slice(0, 2), slice(2, 4)]
+        whole = [slice(0, 4)]
+        load_w(0, 0, halves)
+        load_w(0, 1, halves)
+        load_gs()
+        load_g(0)
+        load_g(1)
+        load_slope(0)
+        load_w(1, 0, whole)
+        load_slope(1)
+        for kg in range(KG):
+            turn_w(0, kg, 0, nc.scalar.copy)
+            turn_w(0, kg, 1, nc.scalar.copy if kg else nc.vector.tensor_copy)
+            quant_w(0, kg)
+        nc.vector.tensor_copy(
+            out=gs[:], in_=gs_raw[:].rearrange("p k n -> p (k n)").rearrange("p (m t) -> p t m", t=4)
+        )
+        order_g(0)
+
+        loads = {
+            0: [(load_g, 2), (load_w, 1, 1, whole), (load_x, 0)],
+            1: [(load_g, 3)],
+            2: [(load_a,), (load_x, 1), (load_w, 2, 0, whole)],
+            3: [(load_x, 2)],
+            4: [(load_w, 2, 1, whole)],
+            5: [(load_x, 3)],
+            8: [(load_acc,)],
+        }
+        w_turns = {0: [(1, 0, 0), (1, 0, 1)], 1: [(1, 1, 0)], 2: [(1, 1, 1)], 3: [(2, 0, 0)], 4: [(2, 0, 1)], 5: [(2, 1, 0)], 6: [(2, 1, 1)]}
+        x_turns = {1: [0], 2: [1], 3: [2], 4: [3], 5: [4], 6: [5], 7: [6, 7]}
+        h_steps = {5: 0, 6: 1, 8: 2, 9: 3}
+        for u in range(12):
+            for item in loads.get(u, []):
+                item[0](*item[1:])
+            if u + 2 < 12:
+                load_slope(u + 2)
+            back(u)
+            for turn in w_turns.get(u, []):
+                turn_w(*turn, nc.scalar.copy)
+            for pair in x_turns.get(u, []):
+                turn_x(pair // 2, pair % 2)
+            if u in h_steps:
+                h_product(h_steps[u])
+            if u == 3:
+                nc.scalar.copy(out=a_grp[:], in_=a_raw[:].rearrange("p k j r -> p k r j"))
+            if u < 3:
+                order_g(u + 1)
+            for c, kg, h in w_turns.get(u - 1, []):
+                if h == 1:
+                    quant_w(c, kg)
+            for pair in x_turns.get(u - 1, []):
+                quant_x(pair // 2, pair % 2)
+            if u == 4:
+                nc.vector.quantize_mx(
+                    out=a_codes[:].bitcast(E4M3), scales=a_scales[:], in_=a_grp[:].rearrange("p k r j -> p (k r j)")
+                )
+            if u > 0:
+                quant_dy(u - 1)
+            if u - 1 in h_steps:
+                quant_h(h_steps[u - 1])
+            mult(u)
+            if u == 10:
+                for g in range(3):
+                    db_pass(0, g)
+            if u == 11:
+                db_pass(0, 3)
+                for g in range(4):
+                    db_pass(1, g)
+                for g in range(3):
+                    db_pass(2, g)
+                combine(0, False)
+                combine(1, False)
+        quant_dy(11)
+        db_pass(2, 3)
+        combine(2, True)

@@ -36,13 +36,11 @@ def tile_lora_up_factor_gradient_e3_kernel(tc, x, a_down, g_words, g_scales, w, 
 
         w_raw = {}
 
-        def load_w(c, kg, halves):
-            if (c, kg) not in w_raw:
-                w_raw[c, kg] = ring.tile([P, 4, KP], BF16, name="w_raw", bufs=4, align_bytes=64)
-            t = w_raw[c, kg]
-            src = w[512 * c : 512 * (c + 1), KP * kg : KP * (kg + 1)].rearrange("(r p) k -> p r k", p=P)
-            for h in halves:
-                nc.sync.dma_start(out=t[:, h, :], in_=src[:, h, :])
+        def load_w(c, h):
+            t = ring.tile([P, 2, O], BF16, name="w_raw", bufs=4, align_bytes=64)
+            src = w[512 * c : 512 * (c + 1), :].rearrange("(m s) k -> m s k", s=4)
+            nc.sync.dma_start(out=t[:], in_=src[:, 2 * h : 2 * h + 2, :])
+            w_raw[c, h] = t
 
         g_flat = g_words.rearrange("k p n t -> k p (n t)")
         g_raw = {}
@@ -55,12 +53,13 @@ def tile_lora_up_factor_gradient_e3_kernel(tc, x, a_down, g_words, g_scales, w, 
 
         x_raw = {}
 
-        def load_x(g):
-            t = ring.tile([P, 4, D], BF16, name="x_raw", bufs=2, align_bytes=64)
+        def load_x(pair):
+            g, h = divmod(pair, 2)
+            t = ring.tile([P, 2, D], BF16, name="x_raw", bufs=4, align_bytes=64)
             src = x[KP * g : KP * (g + 1), :].rearrange("(j t b) d -> b j t d", t=4, b=4)
             for b in range(4):
-                nc.sync.dma_start(out=t[b:P:4, :, :], in_=src[b])
-            x_raw[g] = t
+                nc.sync.dma_start(out=t[b:P:4, :, :], in_=src[b, :, 2 * h : 2 * h + 2, :])
+            x_raw[pair] = t
 
         slopes = {}
 
@@ -104,26 +103,18 @@ def tile_lora_up_factor_gradient_e3_kernel(tc, x, a_down, g_words, g_scales, w, 
         def tr_bank():
             return psum.tile([P, 2, 2, P], F32, name="tr", bufs=4)
 
-        def unscramble(copy, dst, bank):
-            copy(
-                out=dst.rearrange("p n j -> p (n j)").bitcast(F32).rearrange("p (r m u) -> p r m u", r=2, u=2),
-                in_=bank[:].rearrange("p r u m -> p r m u"),
-            )
-
-        def transposes_w(c, kg, h):
-            bank = tr_bank()
-            for r in range(2):
-                words = w_raw[c, kg][:, 2 * h + r, :].bitcast(F32)
-                for u in range(2):
-                    nc.tensor.transpose(bank[:, r, u, :], words[:, u : 256 : 2], ident[:])
-            return bank
-
         w_grp = {}
 
         def turn_w(c, kg, h, copy):
             if h == 0:
                 w_grp[c, kg] = ring.tile([P, 512, 4], BF16, name="w_grp", bufs=3, align_bytes=64)
-            unscramble(copy, w_grp[c, kg][:, 256 * h : 256 * (h + 1), :], transposes_w(c, kg, h))
+            bank = tr_bank()
+            for r in range(2):
+                words = w_raw[c, h][:, r, :].bitcast(F32)
+                for u in range(2):
+                    nc.tensor.transpose(bank[:, r, u, :], words[:, 256 * kg + u : 256 * (kg + 1) : 2], ident[:])
+            dst = w_grp[c, kg][:].rearrange("p n j -> p (n j)").bitcast(F32).rearrange("p (m s) -> p m s", s=8)
+            copy(out=dst[:, :, 4 * h : 4 * h + 4], in_=bank[:].rearrange("p r u m -> p m (r u)"))
 
         def quant_w(c, kg):
             nc.vector.quantize_mx(
@@ -137,14 +128,17 @@ def tile_lora_up_factor_gradient_e3_kernel(tc, x, a_down, g_words, g_scales, w, 
         x_scales = {}
 
         def turn_x(g, h):
-            grp = ring.tile([P, 2, 256, 4], BF16, name="x_grp", bufs=3, align_bytes=64)
+            grp = ring.tile([P, 2, 256, 4], BF16, name="x_grp", bufs=4, align_bytes=64)
             for i in range(2):
                 bank = tr_bank()
-                words = x_raw[g][:, 2 * h + i, :].bitcast(F32)
+                words = x_raw[2 * g + h][:, i, :].bitcast(F32)
                 for kg in range(KG):
                     for u in range(2):
                         nc.tensor.transpose(bank[:, kg, u, :], words[:, 256 * kg + u : 256 * (kg + 1) : 2], ident[:])
-                unscramble(nc.scalar.copy, grp[:, i, :, :], bank)
+                nc.scalar.copy(
+                    out=grp[:, i, :, :].rearrange("p n j -> p (n j)").bitcast(F32).rearrange("p (k m u) -> p k m u", k=2, u=2),
+                    in_=bank[:].rearrange("p k u m -> p k m u"),
+                )
             x_grp[g, h] = grp
 
         def quant_x(g, h):
@@ -266,19 +260,17 @@ def tile_lora_up_factor_gradient_e3_kernel(tc, x, a_down, g_words, g_scales, w, 
                 nc.gpsimd.tensor_tensor(out=res[:], in0=scaled[:], in1=acc_sb[:, cols], op=ADD)
             nc.sync.dma_start(out=out[:, cols], in_=res[:])
 
-        halves = [slice(0, 2), slice(2, 4)]
-        whole = [slice(0, 4)]
-        load_w(0, 0, halves)
-        load_w(0, 1, halves)
+        load_w(0, 0)
+        load_w(0, 1)
         load_gs()
         load_g(0)
-        load_g(1)
         load_slope(0)
-        load_w(1, 0, whole)
+        load_g(1)
         load_slope(1)
+        for h in range(2):
+            turn_w(0, 0, h, nc.scalar.copy)
+            turn_w(0, 1, h, nc.vector.tensor_copy)
         for kg in range(KG):
-            turn_w(0, kg, 0, nc.scalar.copy)
-            turn_w(0, kg, 1, nc.scalar.copy if kg else nc.vector.tensor_copy)
             quant_w(0, kg)
         nc.vector.tensor_copy(
             out=gs[:], in_=gs_raw[:].rearrange("p k n -> p (k n)").rearrange("p (m t) -> p t m", t=4)
@@ -286,22 +278,23 @@ def tile_lora_up_factor_gradient_e3_kernel(tc, x, a_down, g_words, g_scales, w, 
         order_g(0)
 
         loads = {
-            0: [(load_g, 2), (load_w, 1, 1, whole), (load_x, 0)],
-            1: [(load_g, 3)],
-            2: [(load_a,), (load_x, 1), (load_w, 2, 0, whole)],
-            3: [(load_x, 2)],
-            4: [(load_w, 2, 1, whole)],
-            5: [(load_x, 3)],
-            8: [(load_acc,)],
+            0: [(load_g, 2), (load_w, 1, 0), (load_slope, 2)],
+            1: [(load_g, 3), (load_w, 1, 1), (load_slope, 3)],
+            2: [(load_slope, 4), (load_x, 0), (load_a,)],
+            3: [(load_w, 2, 0), (load_x, 1), (load_slope, 5)],
+            4: [(load_x, 2), (load_slope, 6)],
+            5: [(load_w, 2, 1), (load_x, 3), (load_slope, 7)],
+            6: [(load_x, 4), (load_x, 5), (load_slope, 8)],
+            7: [(load_x, 6), (load_slope, 9), (load_acc,)],
+            8: [(load_x, 7), (load_slope, 10)],
+            9: [(load_slope, 11)],
         }
-        w_turns = {0: [(1, 0, 0), (1, 0, 1)], 1: [(1, 1, 0)], 2: [(1, 1, 1)], 3: [(2, 0, 0)], 4: [(2, 0, 1)], 5: [(2, 1, 0)], 6: [(2, 1, 1)]}
-        x_turns = {1: [0], 2: [1], 3: [2], 4: [3], 5: [4], 6: [5], 7: [6, 7]}
-        h_steps = {5: 0, 6: 1, 8: 2, 9: 3}
+        w_turns = {1: [(1, 0, 0), (1, 1, 0)], 2: [(1, 0, 1), (1, 1, 1)], 4: [(2, 0, 0)], 5: [(2, 1, 0)], 6: [(2, 0, 1), (2, 1, 1)]}
+        x_turns = {3: [0], 4: [1], 5: [2], 6: [3], 7: [4, 5], 8: [6, 7]}
+        h_steps = {6: 0, 8: 1, 9: 2, 10: 3}
         for u in range(12):
             for item in loads.get(u, []):
                 item[0](*item[1:])
-            if u + 2 < 12:
-                load_slope(u + 2)
             back(u)
             for turn in w_turns.get(u, []):
                 turn_w(*turn, nc.scalar.copy)

@@ -26,7 +26,7 @@ SCALE = 16.0 / 128.0
 
 def tile_lora_up_factor_gradient_e3_kernel(tc, x, a_down, g_words, g_scales, w, slope, acc, out):
     nc = tc.nc
-    units = [(g, c) for c in range(CHUNKS) for g in range(GROUPS)]
+    units = [(0, 0), (1, 0), (0, 1), (1, 1), (2, 0), (2, 1), (3, 0), (3, 1), (0, 2), (1, 2), (2, 2), (3, 2)]
 
     with ExitStack() as ctx:
         keep = ctx.enter_context(tc.tile_pool(name="keep", bufs=1))
@@ -36,10 +36,12 @@ def tile_lora_up_factor_gradient_e3_kernel(tc, x, a_down, g_words, g_scales, w, 
 
         w_raw = {}
 
-        def load_w(c, h):
-            t = ring.tile([P, 2, O], BF16, name="w_raw", bufs=4, align_bytes=64)
+        def load_w(c, h, pieces=1):
+            t = ring.tile([P, 2, O], BF16, name="w_raw", bufs=3, align_bytes=64)
             src = w[512 * c : 512 * (c + 1), :].rearrange("(m s) k -> m s k", s=4)
-            nc.sync.dma_start(out=t[:], in_=src[:, 2 * h : 2 * h + 2, :])
+            step = 2 // pieces
+            for r in range(0, 2, step):
+                nc.sync.dma_start(out=t[:, r : r + step, :], in_=src[:, 2 * h + r : 2 * h + r + step, :])
             w_raw[c, h] = t
 
         g_flat = g_words.rearrange("k p n t -> k p (n t)")
@@ -63,13 +65,20 @@ def tile_lora_up_factor_gradient_e3_kernel(tc, x, a_down, g_words, g_scales, w, 
 
         slopes = {}
 
-        def load_slope(u):
-            g, c = units[u]
-            t = ring.tile([P, 4, 512], BF16, name="slope_sb", bufs=6, align_bytes=64)
-            src = slope[KP * g : KP * (g + 1), 512 * c : 512 * (c + 1)].rearrange("(j t b) n -> b j t n", t=4, b=4)
+        def load_slope(g, c0, c1):
+            if c0 == 2:
+                t = ring.tile([P, 4, 512], BF16, name="slope_end", bufs=2, align_bytes=64)
+                slopes[g, 2] = t[:, :, :]
+            elif c0 == 0:
+                t = ring.tile([P, 4, 1024], BF16, name="slope_sb", bufs=3, align_bytes=64)
+                slopes[g, 0] = t[:, :, 0:512]
+                slopes[g, 1] = t[:, :, 512:1024]
+            src = slope[KP * g : KP * (g + 1), :].rearrange("(j t b) n -> b j t n", t=4, b=4)
             for b in range(4):
-                nc.sync.dma_start(out=t[b:P:4, :, :], in_=src[b])
-            slopes[u] = t
+                if c1 - c0 == 2:
+                    nc.sync.dma_start(out=t[b:P:4, :, :], in_=src[b, :, :, 0:1024])
+                else:
+                    nc.sync.dma_start(out=slopes[g, c0][b:P:4, :, :], in_=src[b, :, :, 512 * c0 : 512 * c1])
 
         gs_raw = keep.tile([P, KG, T // 4], I32, name="gs_raw", align_bytes=64)
         nc.vector.memset(gs_raw[:], 0)
@@ -128,7 +137,7 @@ def tile_lora_up_factor_gradient_e3_kernel(tc, x, a_down, g_words, g_scales, w, 
         x_scales = {}
 
         def turn_x(g, h):
-            grp = ring.tile([P, 2, 256, 4], BF16, name="x_grp", bufs=4, align_bytes=64)
+            grp = ring.tile([P, 2, 256, 4], BF16, name="x_grp", bufs=3, align_bytes=64)
             for i in range(2):
                 bank = tr_bank()
                 words = x_raw[2 * g + h][:, i, :].bitcast(F32)
@@ -162,10 +171,12 @@ def tile_lora_up_factor_gradient_e3_kernel(tc, x, a_down, g_words, g_scales, w, 
 
         y = {}
 
-        def back(u):
+        def back(u, pass_major, copies):
             g, c = units[u]
             banks = [psum.tile([P, 512], F32, name=f"back{t}", bufs=1) for t in range(4)]
-            for t, kg in [(t, kg) for t in range(4) for kg in range(KG)]:
+            by_bank = [(t, kg) for t in range(4) for kg in range(KG)]
+            by_pass = [(t, kg) for kg in range(KG) for t in range(4)]
+            for t, kg in by_pass if pass_major else by_bank:
                 col = 32 * (GROUPS * kg + g)
                 nc.tensor.matmul_mx(
                     out=banks[t][:],
@@ -178,7 +189,7 @@ def tile_lora_up_factor_gradient_e3_kernel(tc, x, a_down, g_words, g_scales, w, 
                 )
             y[u] = ring.tile([P, P, 4, 4], F32, name="y", bufs=3, align_bytes=64)
             for t in range(4):
-                nc.scalar.copy(out=y[u][:, :, t, :], in_=banks[t][:].rearrange("p (c i) -> p c i", i=4))
+                copies[t % 2](out=y[u][:, :, t, :], in_=banks[t][:].rearrange("p (c i) -> p c i", i=4))
 
         dy = {}
 
@@ -187,7 +198,7 @@ def tile_lora_up_factor_gradient_e3_kernel(tc, x, a_down, g_words, g_scales, w, 
             nc.vector.tensor_tensor(
                 out=dy[u][:].rearrange("p (c i) t -> p c t i", i=4),
                 in0=y[u][:],
-                in1=slopes[u][:].rearrange("p t (c i) -> p c t i", i=4),
+                in1=slopes[units[u]].rearrange("p t (c i) -> p c t i", i=4),
                 op=MULT,
             )
 
@@ -260,58 +271,66 @@ def tile_lora_up_factor_gradient_e3_kernel(tc, x, a_down, g_words, g_scales, w, 
                 nc.gpsimd.tensor_tensor(out=res[:], in0=scaled[:], in1=acc_sb[:, cols], op=ADD)
             nc.sync.dma_start(out=out[:, cols], in_=res[:])
 
-        load_w(0, 0)
-        load_w(0, 1)
+        load_w(0, 0, 2)
         load_gs()
+        load_w(0, 1, 2)
         load_g(0)
-        load_slope(0)
+        load_slope(0, 0, 1)
+        load_w(1, 0)
         load_g(1)
-        load_slope(1)
         for h in range(2):
             turn_w(0, 0, h, nc.scalar.copy)
             turn_w(0, 1, h, nc.vector.tensor_copy)
-        for kg in range(KG):
-            quant_w(0, kg)
-        nc.vector.tensor_copy(
-            out=gs[:], in_=gs_raw[:].rearrange("p k n -> p (k n)").rearrange("p (m t) -> p t m", t=4)
-        )
+            if h == 0:
+                nc.vector.tensor_copy(
+                    out=gs[:], in_=gs_raw[:].rearrange("p k n -> p (k n)").rearrange("p (m t) -> p t m", t=4)
+                )
+        load_w(1, 1)
+        load_slope(1, 0, 2)
+        quant_w(0, 0)
         order_g(0)
+        quant_w(0, 1)
 
         loads = {
-            0: [(load_g, 2), (load_w, 1, 0), (load_slope, 2)],
-            1: [(load_g, 3), (load_w, 1, 1), (load_slope, 3)],
-            2: [(load_slope, 4), (load_x, 0), (load_a,)],
-            3: [(load_w, 2, 0), (load_x, 1), (load_slope, 5)],
-            4: [(load_x, 2), (load_slope, 6)],
-            5: [(load_w, 2, 1), (load_x, 3), (load_slope, 7)],
-            6: [(load_x, 4), (load_x, 5), (load_slope, 8)],
-            7: [(load_x, 6), (load_slope, 9), (load_acc,)],
-            8: [(load_x, 7), (load_slope, 10)],
-            9: [(load_slope, 11)],
+            0: [(load_slope, 0, 1, 2), (load_x, 0)],
+            1: [(load_g, 2), (load_w, 2, 0)],
+            2: [(load_x, 1), (load_slope, 2, 0, 2)],
+            3: [(load_a,), (load_x, 2), (load_g, 3)],
+            4: [(load_w, 2, 1), (load_x, 3), (load_slope, 3, 0, 2)],
+            5: [(load_x, 4), (load_x, 5)],
+            6: [(load_x, 6), (load_slope, 0, 2, 3)],
+            7: [(load_x, 7), (load_slope, 1, 2, 3), (load_acc,)],
+            8: [(load_slope, 2, 2, 3)],
+            9: [(load_slope, 3, 2, 3)],
         }
-        w_turns = {1: [(1, 0, 0), (1, 1, 0)], 2: [(1, 0, 1), (1, 1, 1)], 4: [(2, 0, 0)], 5: [(2, 1, 0)], 6: [(2, 0, 1), (2, 1, 1)]}
-        x_turns = {3: [0], 4: [1], 5: [2], 6: [3], 7: [4, 5], 8: [6, 7]}
-        h_steps = {6: 0, 8: 1, 9: 2, 10: 3}
+        w_turns = {
+            0: [(1, 0, 0), (1, 1, 0), (1, 0, 1), (1, 1, 1)],
+            3: [(2, 0, 0)],
+            4: [(2, 1, 0)],
+            5: [(2, 0, 1)],
+            6: [(2, 1, 1)],
+        }
+        x_turns = {2: [0], 3: [1], 4: [2], 5: [3], 6: [4], 7: [5, 6], 8: [7]}
+        h_steps = {5: 0, 7: 1, 9: 2, 10: 3}
+        g_orders = {0: 1, 3: 2, 5: 3}
         for u in range(12):
             for item in loads.get(u, []):
                 item[0](*item[1:])
-            back(u)
+            back(u, u == 0, [nc.scalar.copy, nc.vector.tensor_copy if u == 0 else nc.scalar.copy])
             for turn in w_turns.get(u, []):
                 turn_w(*turn, nc.scalar.copy)
             for pair in x_turns.get(u, []):
                 turn_x(pair // 2, pair % 2)
-            if u in h_steps:
-                h_product(h_steps[u])
-            if u == 3:
+            if u == 4:
                 nc.scalar.copy(out=a_grp[:], in_=a_raw[:].rearrange("p k j r -> p k r j"))
-            if u < 3:
-                order_g(u + 1)
+            if u in g_orders:
+                order_g(g_orders[u])
             for c, kg, h in w_turns.get(u - 1, []):
                 if h == 1:
                     quant_w(c, kg)
             for pair in x_turns.get(u - 1, []):
                 quant_x(pair // 2, pair % 2)
-            if u == 4:
+            if u == 5:
                 nc.vector.quantize_mx(
                     out=a_codes[:].bitcast(E4M3), scales=a_scales[:], in_=a_grp[:].rearrange("p k r j -> p (k r j)")
                 )
@@ -319,18 +338,16 @@ def tile_lora_up_factor_gradient_e3_kernel(tc, x, a_down, g_words, g_scales, w, 
                 quant_dy(u - 1)
             if u - 1 in h_steps:
                 quant_h(h_steps[u - 1])
+            if u in h_steps:
+                h_product(h_steps[u])
             mult(u)
-            if u == 10:
-                for g in range(3):
-                    db_pass(0, g)
-            if u == 11:
-                db_pass(0, 3)
-                for g in range(4):
-                    db_pass(1, g)
-                for g in range(3):
-                    db_pass(2, g)
-                combine(0, False)
-                combine(1, False)
+        for c in range(2):
+            for g in range(4):
+                db_pass(c, g)
+        for g in range(3):
+            db_pass(2, g)
+        combine(0, False)
+        combine(1, False)
         quant_dy(11)
         db_pass(2, 3)
         combine(2, True)

from contextlib import ExitStack

import concourse.mybir as mybir
from concourse.masks import make_identity

F32 = mybir.dt.float32
BF16 = mybir.dt.bfloat16
I32 = mybir.dt.int32
U32 = mybir.dt.uint32
U8 = mybir.dt.uint8
E4M3 = mybir.dt.float8_e4m3fn_x4
E5M2 = mybir.dt.float8_e5m2_x4
MULT = mybir.AluOpType.mult
ADD = mybir.AluOpType.add

T, D, N, O, R = 2048, 1024, 1536, 1024, 128
FLOPS = 2 * (T * D * R + O * T * N + T * R * N)

P = 128
KP = 512
GROUPS = T // KP
CHUNKS = N // 512
KG = O // KP
SCALE = 16.0 / 128.0


def tile_lora_up_factor_gradient_e3_kernel(tc, x, a_down, g_words, g_scales, w, slope, acc, out):
    nc = tc.nc
    units = [(0, 0), (1, 0), (0, 1), (1, 1), (2, 0), (2, 1), (3, 0), (3, 1), (0, 2), (1, 2), (2, 2), (3, 2)]

    with ExitStack() as ctx:
        keep = ctx.enter_context(tc.tile_pool(name="keep", bufs=1))
        ring = ctx.enter_context(tc.tile_pool(name="ring", bufs=2))
        psum = ctx.enter_context(tc.psum_pool(name="psum", bufs=1))
        ctx.enter_context(tc.manual_schedule())

        w_raw = {}

        def load_w(c, h, pieces=1):
            t = ring.tile([P, 2, O], BF16, name="w_raw", bufs=3, align_bytes=64)
            src = w[512 * c : 512 * (c + 1), :].rearrange("(m s) k -> m s k", s=4)
            step = 2 // pieces
            for r in range(0, 2, step):
                nc.sync.dma_start(out=t[:, r : r + step, :], in_=src[:, 2 * h + r : 2 * h + r + step, :])
            w_raw[c, h] = t

        g_flat = g_words.rearrange("k p n t -> k p (n t)")
        g_raw = {}

        def load_g(g):
            t = ring.tile([P, KG, KP], I32, name="g_raw", bufs=2, align_bytes=64)
            src = g_flat[:, :, 4 * KP * g : 4 * KP * (g + 1)].bitcast(I32).rearrange("k p n -> p k n")
            nc.sync.dma_start(out=t[:], in_=src)
            g_raw[g] = t

        x_raw = {}

        def load_x(pair):
            g, h = divmod(pair, 2)
            t = ring.tile([P, 2, D], BF16, name="x_raw", bufs=4, align_bytes=64)
            src = x[KP * g : KP * (g + 1), :].rearrange("(j t b) d -> b j t d", t=4, b=4)
            for b in range(4):
                nc.sync.dma_start(out=t[b:P:4, :, :], in_=src[b, :, 2 * h : 2 * h + 2, :])
            x_raw[pair] = t

        slopes = {}

        def load_slope(g, c0, c1):
            if c0 == 2:
                t = ring.tile([P, 4, 512], BF16, name="slope_end", bufs=2, align_bytes=64)
                slopes[g, 2] = t[:, :, :]
            elif c0 == 0:
                t = ring.tile([P, 4, 1024], BF16, name="slope_sb", bufs=3, align_bytes=64)
                slopes[g, 0] = t[:, :, 0:512]
                slopes[g, 1] = t[:, :, 512:1024]
            src = slope[KP * g : KP * (g + 1), :].rearrange("(j t b) n -> b j t n", t=4, b=4)
            for b in range(4):
                if c1 - c0 == 2:
                    nc.sync.dma_start(out=t[b:P:4, :, :], in_=src[b, :, :, 0:1024])
                else:
                    nc.sync.dma_start(out=slopes[g, c0][b:P:4, :, :], in_=src[b, :, :, 512 * c0 : 512 * c1])

        gs_raw = keep.tile([P, KG, T // 4], I32, name="gs_raw", align_bytes=64)
        nc.vector.memset(gs_raw[:], 0)
        ident = keep.tile([P, P], F32, name="ident", align_bytes=64)
        make_identity(nc, ident[:])

        def load_gs():
            src = g_scales.bitcast(I32)
            for q in range(4):
                nc.sync.dma_start(
                    out=gs_raw[32 * q : 32 * q + 4, :, :],
                    in_=src[:, 4 * q : 4 * q + 4, :].rearrange("k r n -> r k n"),
                )

        a_raw = keep.tile([P, KG, 4, R], BF16, name="a_raw", align_bytes=64)
        a_grp = keep.tile([P, KG, R, 4], BF16, name="a_grp", align_bytes=64)
        a_codes = keep.tile([P, KG * R], U32, name="a_codes", align_bytes=64)
        a_scales = keep.tile([P, KG * R], U8, name="a_scales", align_bytes=64)
        acc_sb = keep.tile([P, N], BF16, name="acc_sb", align_bytes=64)

        def load_a():
            nc.sync.dma_start(out=a_raw[:], in_=a_down.rearrange("(k p j) r -> p k j r", p=P, j=4))

        def load_acc():
            nc.sync.dma_start(out=acc_sb[:], in_=acc[:, :])

        w_codes = [keep.tile([P, KG, 512], U32, name=f"w_codes{c}", align_bytes=64) for c in range(CHUNKS)]
        w_scales = [keep.tile([P, KG, 512], U8, name=f"w_scales{c}", align_bytes=64) for c in range(CHUNKS)]
        gs = keep.tile([P, 4, KG * GROUPS * 32], I32, name="gs", align_bytes=64)

        def tr_bank():
            return psum.tile([P, 2, 2, P], F32, name="tr", bufs=4)

        w_grp = {}

        def turn_w(c, kg, h, copy):
            if h == 0:
                w_grp[c, kg] = ring.tile([P, 512, 4], BF16, name="w_grp", bufs=3, align_bytes=64)
            bank = tr_bank()
            for r in range(2):
                words = w_raw[c, h][:, r, :].bitcast(F32)
                for u in range(2):
                    nc.tensor.transpose(bank[:, r, u, :], words[:, 256 * kg + u : 256 * (kg + 1) : 2], ident[:])
            dst = w_grp[c, kg][:].rearrange("p n j -> p (n j)").bitcast(F32).rearrange("p (m s) -> p m s", s=8)
            copy(out=dst[:, :, 4 * h : 4 * h + 4], in_=bank[:].rearrange("p r u m -> p m (r u)"))

        def quant_w(c, kg):
            nc.vector.quantize_mx(
                out=w_codes[c][:, kg, :].bitcast(E4M3),
                scales=w_scales[c][:, kg, :],
                in_=w_grp[c, kg][:].rearrange("p n j -> p (n j)"),
            )

        x_grp = {}
        x_codes = {}
        x_scales = {}

        def turn_x(g, h):
            grp = ring.tile([P, 2, 256, 4], BF16, name="x_grp", bufs=3, align_bytes=64)
            for i in range(2):
                bank = tr_bank()
                words = x_raw[2 * g + h][:, i, :].bitcast(F32)
                for kg in range(KG):
                    for u in range(2):
                        nc.tensor.transpose(bank[:, kg, u, :], words[:, 256 * kg + u : 256 * (kg + 1) : 2], ident[:])
                nc.scalar.copy(
                    out=grp[:, i, :, :].rearrange("p n j -> p (n j)").bitcast(F32).rearrange("p (k m u) -> p k m u", k=2, u=2),
                    in_=bank[:].rearrange("p k u m -> p k m u"),
                )
            x_grp[g, h] = grp

        def quant_x(g, h):
            if h == 0:
                x_codes[g] = ring.tile([P, 4, KG * P], U32, name="x_codes", bufs=2, align_bytes=64)
                x_scales[g] = ring.tile([P, 4, KG * P], U8, name="x_scales", bufs=2, align_bytes=64)
            nc.vector.quantize_mx(
                out=x_codes[g][:, 2 * h : 2 * h + 2, :].rearrange("p t c -> p (t c)").bitcast(E4M3),
                scales=x_scales[g][:, 2 * h : 2 * h + 2, :].rearrange("p t c -> p (t c)"),
                in_=x_grp[g, h][:].rearrange("p i n j -> p (i n j)"),
            )

        g_codes = {}

        def order_g(g):
            g_codes[g] = keep.tile([P, 4, KG * P], I32, name=f"g_codes{g}", align_bytes=64)
            nc.vector.tensor_copy(
                out=g_codes[g][:].rearrange("p t (kj b) -> p t kj b", b=4),
                in_=g_raw[g][:].rearrange("p k n -> p (k n)").rearrange("p (kj t b) -> p t kj b", t=4, b=4),
            )

        y = {}

        def back(u, pass_major, copies):
            g, c = units[u]
            banks = [psum.tile([P, 512], F32, name=f"back{t}", bufs=1) for t in range(4)]
            by_bank = [(t, kg) for t in range(4) for kg in range(KG)]
            by_pass = [(t, kg) for kg in range(KG) for t in range(4)]
            for t, kg in by_pass if pass_major else by_bank:
                col = 32 * (GROUPS * kg + g)
                nc.tensor.matmul_mx(
                    out=banks[t][:],
                    lhsT=g_codes[g][:, t, P * kg : P * (kg + 1)].bitcast(E5M2),
                    lhsT_scale=gs[:, t, col : col + 32].bitcast(U8),
                    rhs=w_codes[c][:, kg, :].bitcast(E4M3),
                    rhs_scale=w_scales[c][:, kg, :],
                    start=(kg == 0),
                    stop=(kg == KG - 1),
                )
            y[u] = ring.tile([P, P, 4, 4], F32, name="y", bufs=3, align_bytes=64)
            for t in range(4):
                copies[t % 2](out=y[u][:, :, t, :], in_=banks[t][:].rearrange("p (c i) -> p c i", i=4))

        dy = {}

        def mult(u):
            dy[u] = ring.tile([P, 512, 4], BF16, name="dy", bufs=3, align_bytes=64)
            nc.vector.tensor_tensor(
                out=dy[u][:].rearrange("p (c i) t -> p c t i", i=4),
                in0=y[u][:],
                in1=slopes[units[u]].rearrange("p t (c i) -> p c t i", i=4),
                op=MULT,
            )

        dy_codes = {}
        dy_scales = {}

        def quant_dy(u):
            dy_codes[u] = keep.tile([P, 512], U32, name=f"dy_codes{u}", align_bytes=64)
            dy_scales[u] = keep.tile([P, 512], U8, name=f"dy_scales{u}", align_bytes=64)
            nc.vector.quantize_mx(
                out=dy_codes[u][:].bitcast(E5M2),
                scales=dy_scales[u][:],
                in_=dy[u][:].rearrange("p n t -> p (n t)"),
            )

        h_grp = {}
        h_codes = {}
        h_scales = {}

        def h_product(g):
            bank = psum.tile([P, 4, R], F32, name="tr", bufs=4)
            for t in range(4):
                for kg in range(KG):
                    cols = slice(P * kg, P * (kg + 1))
                    nc.tensor.matmul_mx(
                        out=bank[:, t, :],
                        lhsT=x_codes[g][:, t, cols].bitcast(E4M3),
                        lhsT_scale=x_scales[g][:, t, cols],
                        rhs=a_codes[:, cols].bitcast(E4M3),
                        rhs_scale=a_scales[:, cols],
                        start=(kg == 0),
                        stop=(kg == KG - 1),
                    )
            h_grp[g] = ring.tile([P, R, 4], BF16, name="h_grp", bufs=2, align_bytes=64)
            nc.scalar.copy(out=h_grp[g][:], in_=bank[:].rearrange("p t r -> p r t"))

        def quant_h(g):
            h_codes[g] = keep.tile([P, R], U32, name=f"h_codes{g}", align_bytes=64)
            h_scales[g] = keep.tile([P, R], U8, name=f"h_scales{g}", align_bytes=64)
            nc.vector.quantize_mx(
                out=h_codes[g][:].bitcast(E4M3), scales=h_scales[g][:], in_=h_grp[g][:].rearrange("p r t -> p (r t)")
            )

        db = {}

        def db_pass(c, g):
            if g == 0:
                db[c] = psum.tile([P, 512], F32, name="tr", bufs=4)
            u = units.index((g, c))
            nc.tensor.matmul_mx(
                out=db[c][:],
                lhsT=h_codes[g][:].bitcast(E4M3),
                lhsT_scale=h_scales[g][:],
                rhs=dy_codes[u][:].bitcast(E5M2),
                rhs_scale=dy_scales[u][:],
                start=(g == 0),
                stop=(g == GROUPS - 1),
            )

        def combine(c, on_vector):
            cols = slice(512 * c, 512 * (c + 1))
            res = ring.tile([P, 512], F32, name="res", bufs=3, align_bytes=64)
            if on_vector:
                nc.vector.scalar_tensor_tensor(
                    out=res[:], in0=db[c][:], scalar=SCALE, in1=acc_sb[:, cols], op0=MULT, op1=ADD
                )
            else:
                scaled = ring.tile([P, 512], F32, name="scaled", bufs=2, align_bytes=64)
                nc.scalar.mul(scaled[:], db[c][:], SCALE)
                nc.gpsimd.tensor_tensor(out=res[:], in0=scaled[:], in1=acc_sb[:, cols], op=ADD)
            nc.sync.dma_start(out=out[:, cols], in_=res[:])

        load_w(0, 0, 2)
        load_gs()
        load_w(0, 1, 2)
        load_g(0)
        load_slope(0, 0, 1)
        load_w(1, 0)
        load_g(1)
        for h in range(2):
            turn_w(0, 0, h, nc.scalar.copy)
            turn_w(0, 1, h, nc.vector.tensor_copy)
            if h == 0:
                nc.vector.tensor_copy(
                    out=gs[:], in_=gs_raw[:].rearrange("p k n -> p (k n)").rearrange("p (m t) -> p t m", t=4)
                )
        load_w(1, 1)
        load_slope(1, 0, 2)
        quant_w(0, 0)
        order_g(0)
        quant_w(0, 1)

        loads = {
            0: [(load_slope, 0, 1, 2), (load_x, 0)],
            1: [(load_g, 2), (load_w, 2, 0)],
            2: [(load_x, 1), (load_slope, 2, 0, 2)],
            3: [(load_a,), (load_x, 2), (load_g, 3)],
            4: [(load_w, 2, 1), (load_x, 3), (load_slope, 3, 0, 2)],
            5: [(load_x, 4), (load_x, 5)],
            6: [(load_x, 6), (load_slope, 0, 2, 3)],
            7: [(load_x, 7), (load_slope, 1, 2, 3), (load_acc,)],
            8: [(load_slope, 2, 2, 3)],
            9: [(load_slope, 3, 2, 3)],
        }
        w_turns = {
            0: [(1, 0, 0), (1, 1, 0), (1, 0, 1), (1, 1, 1)],
            3: [(2, 0, 0)],
            4: [(2, 1, 0)],
            5: [(2, 0, 1)],
            6: [(2, 1, 1)],
        }
        x_turns = {2: [0], 3: [1], 4: [2], 5: [3], 6: [4], 7: [5, 6], 8: [7]}
        h_steps = {5: 0, 7: 1, 9: 2, 10: 3}
        g_orders = {0: 1, 3: 2, 5: 3}
        for u in range(12):
            for item in loads.get(u, []):
                item[0](*item[1:])
            back(u, u == 0, [nc.scalar.copy, nc.vector.tensor_copy if u == 0 else nc.scalar.copy])
            for turn in w_turns.get(u, []):
                turn_w(*turn, nc.scalar.copy)
            for pair in x_turns.get(u, []):
                turn_x(pair // 2, pair % 2)
            if u == 4:
                nc.scalar.copy(out=a_grp[:], in_=a_raw[:].rearrange("p k j r -> p k r j"))
            if u in g_orders:
                order_g(g_orders[u])
            for c, kg, h in w_turns.get(u - 1, []):
                if h == 1:
                    quant_w(c, kg)
            for pair in x_turns.get(u - 1, []):
                quant_x(pair // 2, pair % 2)
            if u == 5:
                nc.vector.quantize_mx(
                    out=a_codes[:].bitcast(E4M3), scales=a_scales[:], in_=a_grp[:].rearrange("p k r j -> p (k r j)")
                )
            if u > 0:
                quant_dy(u - 1)
            if u - 1 in h_steps:
                quant_h(h_steps[u - 1])
            if u in h_steps:
                h_product(h_steps[u])
            mult(u)
        for c in range(2):
            for g in range(4):
                db_pass(c, g)
        for g in range(3):
            db_pass(2, g)
        combine(0, False)
        combine(1, False)
        quant_dy(11)
        db_pass(2, 3)
        combine(2, True)
